import numpy as np
import ml_dtypes


def mxq(x, axis, fmt="e4m3"):
    dtype, down = {"e4m3": (ml_dtypes.float8_e4m3fn, 7), "e5m2": (ml_dtypes.float8_e5m2, 14)}[fmt]
    v = np.moveaxis(np.asarray(x, np.float32).astype(ml_dtypes.bfloat16).astype(np.float64), axis, -1)
    blocks = v.reshape(v.shape[:-1] + (-1, 32))
    amax = np.abs(blocks).max(-1, keepdims=True)
    byte = np.maximum(np.where(amax > 0, np.frexp(amax)[1] - 1 + 127, 0) - down, 1)
    scale = np.exp2(byte - 127.0)
    codes = (blocks / scale).astype(np.float32).astype(dtype).astype(np.float64)
    return np.moveaxis((codes * scale).reshape(v.shape), -1, axis)


WIDE = False


def mx_kscale(k):
    if not WIDE:
        return np.ones(k)
    levels = np.array([10, -10, 5, -5, 0])
    if k % 512:
        return np.exp2(np.random.permutation(np.resize(levels, k // 32))).repeat(32)
    a = np.empty((k // 512, 16))
    for p in range(k // 512):
        a[p, :8] = np.random.permutation(np.resize(levels, 8))
        for g in range(8):
            far = levels[np.abs(levels - a[p, g]) >= 10]
            a[p, g + 8] = far[np.random.randint(len(far))]
    return np.exp2(a.ravel()).repeat(32)


BF16 = ml_dtypes.bfloat16


def bf(x):
    return np.asarray(x, np.float32).astype(BF16)


def f64(x):
    return np.asarray(x).astype(np.float64)


E2M1 = np.array([0.0, 0.5, 1.0, 1.5, 2.0, 3.0, 4.0, 6.0, -0.0, -0.5, -1.0, -1.5, -2.0, -3.0, -4.0, -6.0])


def pack_weight(w, fmt):
    k, n = w.shape
    w = f64(bf(w)).reshape(k // 32, 32, n)
    amax = np.abs(w).max(1)
    if fmt == "e4m3":
        byte = np.frexp(amax)[1] - 1 + 127 - 7
    else:
        mant, ex = np.frexp(amax / 6.0)
        byte = np.where(mant > 0.5, ex, ex - 1) + 127
    byte = np.clip(np.where(amax > 0, byte, 1), 1, 254)
    scaled = (w * np.exp2(127.0 - byte)[:, None, :]).reshape(k, n).astype(np.float32)
    by_word = np.ascontiguousarray(scaled.reshape(k // 512, 128, 4, n).transpose(0, 1, 3, 2))
    if fmt == "e4m3":
        words = by_word.astype(ml_dtypes.float8_e4m3fn).view(np.uint8)
    else:
        c = by_word.astype(ml_dtypes.float4_e2m1fn).view(np.uint8) & 0xF
        words = c[..., 0::2] | (c[..., 1::2] << 4)
    return np.ascontiguousarray(words), np.ascontiguousarray(byte.astype(np.uint8).reshape(k // 512, 16, n))


def unpack_weight(words, scales, fmt):
    g, p, n, _ = words.shape
    if fmt == "e4m3":
        vals = np.ascontiguousarray(words).view(ml_dtypes.float8_e4m3fn).astype(np.float64)
    else:
        nib = np.empty((g, p, n, 4), np.uint8)
        nib[..., 0::2] = words & 0xF
        nib[..., 1::2] = words >> 4
        vals = E2M1[nib]
    vals = vals * np.repeat(np.exp2(scales.astype(np.float64) - 127.0), 8, axis=1)[..., None]
    return vals.transpose(0, 1, 3, 2).reshape(g * 512, n)
def pack4(w):
    words, scales = pack_weight(w, "e2m1")
    return words.reshape(words.shape[0], 128, -1), scales


def unpack4(words, scales):
    return unpack_weight(words.reshape(words.shape[0], 128, -1, 2), scales, "e2m1")


M, N, D, F, C = 1024, 2048, 1024, 512, 512

SPREAD = 0.7
JITTER = 0.3


def setup_inputs():
    s = mx_kscale(D)
    u = mx_kscale(F)
    t = mx_kscale(N)
    a_words, a_scales = pack4(np.random.standard_normal((D, M)) * s[:, None])
    b_words, b_scales = pack4(SPREAD * np.random.standard_normal((D, N)) / np.sqrt(D) / s[:, None])
    return {"a_words": a_words, "a_scales": a_scales,
            "b_words": b_words, "b_scales": b_scales,
            "gamma": bf(np.exp(JITTER * np.random.standard_normal(N)) / np.sqrt(N) * t),
            "rho": bf(np.exp(JITTER * np.random.standard_normal(M))),
            "x": bf(np.random.standard_normal((N, F)) * u / t[:, None]),
            "w": bf(np.random.standard_normal((F, C)) / np.sqrt(F) / u[:, None])}


def reference(a_words, a_scales, b_words, b_scales, gamma, rho, x, w):
    gram = unpack4(a_words, a_scales).T @ unpack4(b_words, b_scales)
    weights = np.exp(gram) * f64(gamma)
    v = mxq(f64(x), 1, "e4m3") @ mxq(f64(w), 0, "e4m3")
    avg = mxq(weights, 1, "e4m3") @ mxq(v, 0, "e4m3")
    return avg * f64(rho)[:, None]

@@ -1,0 +1,363 @@
+import math
+from contextlib import ExitStack
+
+import concourse.mybir as mybir
+from concourse.masks import make_identity
+
+M, N, D, F, C = 1024, 2048, 1024, 512, 512
+FLOPS = 2 * (M * N * D + N * F * C + M * N * C)
+
+F32 = mybir.dt.float32
+BF16 = mybir.dt.bfloat16
+I32 = mybir.dt.int32
+U32 = mybir.dt.uint32
+U8 = mybir.dt.uint8
+E4M3 = mybir.dt.float8_e4m3fn_x4
+E2M1 = mybir.dt.float4_e2m1fn_x4
+ALU = mybir.AluOpType
+ACT = mybir.ActivationFunctionType
+
+P = 128
+JG = N // 512
+HALF = 512
+DG = D // 512
+
+
+def tile_balanced_nonlocal_means_s12_kernel(
+    tc, a_words, a_scales, b_words, b_scales, gamma, rho, x, w, out
+):
+    nc = tc.nc
+    with ExitStack() as ctx:
+        keep = ctx.enter_context(tc.tile_pool(name="keep", bufs=1))
+        work = ctx.enter_context(tc.tile_pool(name="work", bufs=3))
+        psum = ctx.enter_context(tc.psum_pool(name="psum", bufs=4))
+        ctx.enter_context(tc.manual_schedule())
+
+        def kept(name, shape, dtype):
+            return keep.tile(shape, dtype, name=name, tag=name, align_bytes=64)
+
+        a_codes = kept("a_codes", [P, DG, 2 * M], U8)
+        a_plane = kept("a_plane", [P, DG, M], U8)
+        b_plane_raw = kept("b_plane_raw", [P, DG, N], U8)
+        b_raw = [kept("b_raw%d" % g, [P, DG, 1024], U8) for g in range(JG)]
+        b_codes = [kept("b_codes%d" % g, [P, DG, 1024], U8) for g in range(JG)]
+        b_plane = [kept("b_plane%d" % g, [P, DG, 512], U8) for g in range(JG)]
+        x_raw = [kept("x_raw%d" % g, [P, 4, F], BF16) for g in range(JG)]
+        w_raw = kept("w_raw", [P, 4, C], BF16)
+        w_grp = kept("w_grp", [P, C, 4], BF16)
+        w_codes = kept("w_codes", [P, C], U32)
+        w_plane = kept("w_plane", [P, C], U8)
+        x_codes = [kept("x_codes%d" % g, [P, 512], U32) for g in range(JG)]
+        x_plane = [kept("x_plane%d" % g, [P, 512], U8) for g in range(JG)]
+        v_codes = [kept("v_codes%d" % g, [P, C], U32) for g in range(JG)]
+        v_plane = [kept("v_plane%d" % g, [P, C], U8) for g in range(JG)]
+        e_codes = [kept("e_codes%d" % s, [P, HALF], U32) for s in range(2 * JG)]
+        e_plane = [kept("e_plane%d" % s, [P, HALF], U8) for s in range(2 * JG)]
+        g_row = kept("g_row", [JG, 512], BF16)
+        vec_rows = kept("vec_rows", [P, 4, P], BF16)
+        rho_rows = kept("rho_rows", [P, P], BF16)
+        id_bf = kept("id_bf", [P, P], BF16)
+        id_f = kept("id_f", [P, P], F32)
+        dummy = kept("dummy", [P, 1], F32)
+        gam = kept("gam", [P, 4, JG], F32)
+        mant = kept("mant", [P, 4, JG], I32)
+        expo = kept("expo", [P, 4, JG], I32)
+        expo_ln = kept("expo_ln", [P, 4, JG], F32)
+        mant_ln = kept("mant_ln", [P, 4, JG], F32)
+        ln_gam = kept("ln_gam", [P, 4, JG], F32)
+        sgn2 = kept("sgn2", [P, JG, 4], F32)
+        sgn = kept("sgn", [P, JG, 4], F32)
+        rho_col = kept("rho_col", [P, M // P], F32)
+
+        def load_b(g):
+            nc.sync.dma_start(
+                out=b_raw[g][:].bitcast(I32),
+                in_=b_words.rearrange("d p n -> p d n")[:, :, g * 1024 : (g + 1) * 1024].bitcast(I32),
+            )
+
+        def load_a(h):
+            nc.sync.dma_start(
+                out=a_codes[:, :, h * 1024 : (h + 1) * 1024].bitcast(I32),
+                in_=a_words.rearrange("d p n -> p d n")[:, :, h * 1024 : (h + 1) * 1024].bitcast(I32),
+            )
+
+        def load_x(g):
+            nc.sync.dma_start(out=x_raw[g][:], in_=x.rearrange("(g m b) f -> g m b f", g=JG, b=4)[g])
+
+        nc.gpsimd.dma_start(out=g_row[:], in_=gamma.rearrange("(g n) -> g n", g=JG))
+        nc.vector.memset(b_plane_raw[:].bitcast(I32), 0)
+        make_identity(nc, id_bf[:])
+        nc.vector.memset(a_plane[:].bitcast(I32), 0)
+        nc.vector.memset(vec_rows[:], 0.0)
+        nc.vector.memset(dummy[:], 1.0)
+        nc.vector.memset(rho_rows[:], 0.0)
+
+        def load_plane(queue, plane, rows, q):
+            queue.dma_start(
+                out=plane[32 * q : 32 * q + 4, :, :].bitcast(I32),
+                in_=rows[:, 4 * q : 4 * q + 4, :].rearrange("d r n -> r d n").bitcast(I32),
+            )
+
+        load_x(0)
+        load_b(0)
+        load_a(0)
+        for q in range(4):
+            load_plane(nc.scalar, b_plane_raw, b_scales, q)
+        load_plane(nc.scalar, a_plane, a_scales, 0)
+        for q in range(1, 4):
+            load_plane(nc.gpsimd, a_plane, a_scales, q)
+        nc.gpsimd.dma_start(out=rho_rows[0:8, :], in_=rho.rearrange("(i p) -> i p", p=P))
+        nc.sync.dma_start(out=w_raw[:], in_=w.rearrange("(p j) c -> p j c", j=4))
+        load_b(1)
+        load_b(2)
+        load_b(3)
+        load_x(1)
+        load_x(2)
+        load_x(3)
+        load_a(1)
+
+        nc.scalar.activation(out=mant_ln[:, 0, 0:1], in_=dummy[:], func=ACT.Ln)
+        nc.vector.tensor_copy(out=id_f[:], in_=id_bf[:])
+
+        def arrange_b(g):
+            for d in range(DG):
+                nc.vector.tensor_copy(
+                    out=b_codes[g][:, d, :].bitcast(I32).rearrange("p (t s w) -> p t s w", t=4, w=2),
+                    in_=b_raw[g][:, d, :].bitcast(I32).rearrange("p (s t w) -> p t s w", t=4, w=2),
+                )
+            nc.vector.tensor_copy(
+                out=b_plane[g][:].bitcast(I32).rearrange("p d (t s) -> p d t s", t=4),
+                in_=b_plane_raw[:, :, g * 512 : (g + 1) * 512].bitcast(I32).rearrange("p d (s t) -> p d t s", t=4),
+            )
+
+        x_grp = {}
+        e_bf = {}
+        e_grp = {}
+        v_grp = {}
+        o_bank = {}
+
+        def turn_x(g, copy):
+            grp = work.tile([P, 512, 4], BF16, name="x_grp", tag="x_grp", bufs=2, align_bytes=64)
+            x_grp[g] = grp
+            words = grp[:].rearrange("p c j -> p (c j)").bitcast(F32)
+            banks = []
+            for k in range(2):
+                bank = psum.tile([P, 4, P], F32, name="xt", tag="m", bufs=4)
+                banks.append(bank)
+                for bl in range(2):
+                    for u in range(2):
+                        nc.tensor.transpose(
+                            bank[:, 2 * bl + u, :], x_raw[g][:, 2 * k + bl, :].bitcast(F32)[:, u::2], id_f[:]
+                        )
+            for k in range(2):
+                copy(
+                    out=words.rearrange("p (t s e) -> p t s e", t=4, e=8)[:, :, :, 4 * k : 4 * k + 4],
+                    in_=banks[k][:].rearrange("p e (s t) -> p t s e", t=4),
+                )
+
+        def quant_x(g):
+            nc.vector.quantize_mx(
+                out=x_codes[g][:].bitcast(E4M3), scales=x_plane[g][:], in_=x_grp[g][:].rearrange("p c j -> p (c j)")
+            )
+
+        def weigh(s, t):
+            h, g = divmod(s, JG)
+            bank = psum.tile([P, HALF], F32, name="gram", tag="m", bufs=4)
+            for d in range(DG):
+                nc.tensor.matmul_mx(
+                    out=bank[:],
+                    lhsT=b_codes[g][:, d, 256 * t : 256 * (t + 1)].bitcast(E2M1),
+                    lhsT_scale=b_plane[g][:, d, P * t : P * (t + 1)],
+                    rhs=a_codes[:, d, 1024 * h : 1024 * (h + 1)].bitcast(E2M1),
+                    rhs_scale=a_plane[:, d, HALF * h : HALF * (h + 1)],
+                    start=(d == 0),
+                    stop=(d == DG - 1),
+                )
+            if t == 0:
+                e_bf[s] = work.tile([P, 4, HALF], BF16, name="e_bf", tag="e_bf", bufs=8, align_bytes=64)
+            nc.scalar.activation(out=e_bf[s][:, t, :], in_=bank[:], func=ACT.Exp, bias=ln_gam[:, t, g : g + 1])
+
+        def interleave(s, part):
+            if part == 0:
+                e_grp[s] = work.tile([P, HALF, 4], BF16, name="e_grp", tag="e_grp", bufs=3, align_bytes=64)
+            cols = slice(part * 256, (part + 1) * 256)
+            nc.vector.tensor_copy(
+                out=e_grp[s][:, cols, :].rearrange("p (c i) t -> p c t i", i=4),
+                in_=e_bf[s][:, :, cols].rearrange("p t (c i) -> p c t i", i=4),
+            )
+
+        def quant_e(s):
+            nc.vector.quantize_mx(
+                out=e_codes[s][:].bitcast(E4M3), scales=e_plane[s][:], in_=e_grp[s][:].rearrange("p c t -> p (c t)")
+            )
+
+        def project(g, cq):
+            bank = psum.tile([P, 4, P], F32, name="val", tag="m", bufs=4)
+            cols = slice(P * cq, P * (cq + 1))
+            for t in range(4):
+                nc.tensor.matmul_mx(
+                    out=bank[:, t, :],
+                    lhsT=x_codes[g][:, P * t : P * (t + 1)].bitcast(E4M3),
+                    lhsT_scale=x_plane[g][:, P * t : P * (t + 1)],
+                    rhs=w_codes[:, cols].bitcast(E4M3),
+                    rhs_scale=w_plane[:, cols],
+                    start=True,
+                    stop=True,
+                )
+            if cq == 0:
+                v_grp[g] = work.tile([P, C, 4], BF16, name="v_grp", tag="v_grp", bufs=2, align_bytes=64)
+            nc.vector.tensor_tensor(
+                out=v_grp[g][:, cols, :],
+                in0=bank[:].rearrange("p t c -> p c t"),
+                in1=sgn[:, g : g + 1, :].to_broadcast([P, P, 4]),
+                op=ALU.mult,
+            )
+
+        def quant_v(g):
+            nc.vector.quantize_mx(
+                out=v_codes[g][:].bitcast(E4M3), scales=v_plane[g][:], in_=v_grp[g][:].rearrange("p c t -> p (c t)")
+            )
+
+        def average(h, i, g):
+            if g == 0:
+                o_bank[h, i] = psum.tile([P, C], F32, name="avg", tag=("o", "m")[h], bufs=4)
+            s = h * JG + g
+            nc.tensor.matmul_mx(
+                out=o_bank[h, i][:],
+                lhsT=e_codes[s][:, P * i : P * (i + 1)].bitcast(E4M3),
+                lhsT_scale=e_plane[s][:, P * i : P * (i + 1)],
+                rhs=v_codes[g][:].bitcast(E4M3),
+                rhs_scale=v_plane[g][:],
+                start=(g == 0),
+                stop=(g == JG - 1),
+            )
+
+        def finish(h, i, on_vector):
+            k = 4 * h + i
+            res = work.tile([P, C], F32, name="res", tag="res", bufs=4)
+            if on_vector:
+                nc.vector.tensor_scalar_mul(out=res[:], in0=o_bank[h, i][:], scalar1=rho_col[:, k : k + 1])
+            else:
+                nc.scalar.activation(out=res[:], in_=o_bank[h, i][:], func=ACT.Copy, scale=rho_col[:, k : k + 1])
+            nc.sync.dma_start(out=out[P * k : P * (k + 1), :], in_=res[:])
+
+        nc.vector.tensor_copy(
+            out=vec_rows[0:JG, :, :].rearrange("g t (s b) -> g t s b", b=4),
+            in_=g_row[:].rearrange("g (s t b) -> g t s b", t=4, b=4),
+        )
+        vec_t = psum.tile([P, 4, P], BF16, name="vec_t", tag="m", bufs=4)
+        for t in range(4):
+            nc.tensor.transpose(vec_t[:, t, :], vec_rows[:, t, :], id_bf[:])
+        nc.vector.tensor_copy(out=gam[:], in_=vec_t[:, :, 0:JG])
+        bits = gam[:].bitcast(I32)
+        nc.vector.tensor_scalar(
+            out=mant[:], in0=bits, scalar1=0x007FFFFF, scalar2=0x3F800000, op0=ALU.bitwise_and, op1=ALU.bitwise_or
+        )
+        nc.vector.tensor_scalar(
+            out=expo[:], in0=bits, scalar1=23, scalar2=0xFF, op0=ALU.logical_shift_right, op1=ALU.bitwise_and
+        )
+        nc.scalar.activation(out=mant_ln[:], in_=mant[:].bitcast(F32), func=ACT.Ln)
+        nc.scalar.activation(out=dummy[:], in_=dummy[:], func=ACT.Exp)
+        turn_x(0, nc.vector.tensor_copy)
+        arrange_b(0)
+        nc.vector.tensor_scalar(
+            out=expo_ln[:], in0=expo[:], scalar1=-127.0, scalar2=math.log(2.0), op0=ALU.add, op1=ALU.mult
+        )
+        nc.vector.tensor_scalar(
+            out=sgn2[:], in0=gam[:].rearrange("p t g -> p g t"), scalar1=0.0, scalar2=2.0, op0=ALU.is_ge, op1=ALU.mult
+        )
+        nc.vector.tensor_tensor(out=ln_gam[:], in0=mant_ln[:], in1=expo_ln[:], op=ALU.add)
+        nc.vector.tensor_scalar_add(out=sgn[:], in0=sgn2[:], scalar1=-1.0)
+
+
+        def weights_w():
+            nc.vector.tensor_copy(
+                out=w_grp[:].rearrange("p (c i) j -> p c j i", i=4), in_=w_raw[:].rearrange("p j (c i) -> p c j i", i=4)
+            )
+
+        def quant_w():
+            nc.vector.quantize_mx(
+                out=w_codes[:].bitcast(E4M3), scales=w_plane[:], in_=w_grp[:].rearrange("p c j -> p (c j)")
+            )
+        for t in range(4):
+            weigh(0, t)
+        quant_x(0)
+        weights_w()
+        arrange_b(1)
+        quant_w()
+        turn_x(1, nc.scalar.copy)
+        arrange_b(2)
+        rho_t = psum.tile([P, P], BF16, name="rho_t", tag="m", bufs=4)
+        nc.tensor.transpose(rho_t[:], rho_rows[:], id_bf[:])
+        nc.vector.tensor_copy(out=rho_col[:], in_=rho_t[:, 0:8])
+        interleave(0, 0)
+        for t in range(4):
+            weigh(1, t)
+        interleave(0, 1)
+        arrange_b(3)
+        quant_x(1)
+        turn_x(2, nc.scalar.copy)
+        quant_e(0)
+        for t in range(4):
+            weigh(2, t)
+            project(0, t)
+            if t == 0:
+                interleave(1, 0)
+            if t == 1:
+                interleave(1, 1)
+        quant_x(2)
+        quant_v(0)
+        turn_x(3, nc.scalar.copy)
+        for t in range(4):
+            weigh(3, t)
+            project(1, t)
+            if t == 0:
+                quant_e(1)
+        quant_x(3)
+        quant_v(1)
+        interleave(2, 0)
+        for t in range(4):
+            weigh(4, t)
+            project(2, t)
+        interleave(2, 1)
+        for t in range(4):
+            weigh(5, t)
+            project(3, t)
+        quant_v(2)
+        quant_e(2)
+        quant_v(3)
+        interleave(3, 0)
+        interleave(3, 1)
+        for t in range(4):
+            weigh(6, t)
+            average(0, t, 0)
+        interleave(4, 0)
+        quant_e(3)
+        for t in range(4):
+            average(0, t, 1)
+        interleave(4, 1)
+        for t in range(4):
+            weigh(7, t)
+            average(0, t, 2)
+        interleave(5, 0)
+        quant_e(4)
+        interleave(5, 1)
+        interleave(6, 0)
+        quant_e(5)
+        interleave(6, 1)
+        for t in range(4):
+            average(0, t, 3)
+            finish(0, t, False)
+        interleave(7, 0)
+        quant_e(6)
+        interleave(7, 1)
+        for i in range(4):
+            for g in range(3):
+                average(1, i, g)
+            if i == 1:
+                quant_e(7)
+            if i > 0:
+                average(1, i - 1, 3)
+                finish(1, i - 1, i % 2 == 1)
+        average(1, 3, 3)
+        finish(1, 3, False)

@@ -5,6 +5,139 @@ import concourse.mybir as mybir
 from concourse.masks import make_identity
 
 M, N, D, F, C = 1024, 2048, 1024, 512, 512
+PLAN = [
+    ("T", 0,),
+    ("rho",),
+    ("arr", 0,),
+    ("G", 0, 0,),
+    ("qx", 0,),
+    ("arr", 1,),
+    ("G", 0, 1,),
+    ("G", 0, 2,),
+    ("G", 0, 3,),
+    ("wi",),
+    ("G", 1, 0,),
+    ("G", 1, 1,),
+    ("il", 0, 0,),
+    ("G", 1, 2,),
+    ("G", 1, 3,),
+    ("arr", 2,),
+    ("T", 1,),
+    ("arr", 3,),
+    ("T", 2,),
+    ("wq",),
+    ("il", 1, 0,),
+    ("il", 0, 1,),
+    ("qx", 1,),
+    ("V", 0, 0,),
+    ("G", 2, 0,),
+    ("il", 1, 1,),
+    ("G", 2, 1,),
+    ("V", 1, 0,),
+    ("V", 1, 1,),
+    ("qe", 1,),
+    ("G", 3, 0,),
+    ("V", 0, 1,),
+    ("G", 2, 2,),
+    ("qx", 2,),
+    ("G", 2, 3,),
+    ("V", 0, 2,),
+    ("V", 1, 2,),
+    ("V", 0, 3,),
+    ("T", 3,),
+    ("G", 4, 0,),
+    ("qe", 0,),
+    ("G", 3, 1,),
+    ("qv", 0,),
+    ("il", 2, 0,),
+    ("G", 3, 2,),
+    ("qx", 3,),
+    ("V", 1, 3,),
+    ("G", 3, 3,),
+    ("V", 2, 0,),
+    ("qv", 1,),
+    ("G", 4, 1,),
+    ("V", 2, 1,),
+    ("V", 3, 0,),
+    ("G", 4, 2,),
+    ("il", 3, 0,),
+    ("G", 4, 3,),
+    ("O", 0, 2, 0,),
+    ("V", 2, 2,),
+    ("O", 0, 3, 0,),
+    ("V", 3, 1,),
+    ("il", 2, 1,),
+    ("G", 5, 0,),
+    ("V", 3, 2,),
+    ("il", 4, 0,),
+    ("O", 0, 2, 1,),
+    ("O", 0, 0, 0,),
+    ("G", 6, 0,),
+    ("V", 2, 3,),
+    ("G", 5, 1,),
+    ("O", 0, 1, 0,),
+    ("il", 3, 1,),
+    ("O", 0, 0, 1,),
+    ("G", 7, 0,),
+    ("G", 5, 2,),
+    ("G", 5, 3,),
+    ("qv", 2,),
+    ("il", 4, 1,),
+    ("qe", 2,),
+    ("V", 3, 3,),
+    ("il", 5, 0,),
+    ("G", 6, 1,),
+    ("il", 5, 1,),
+    ("qv", 3,),
+    ("G", 6, 2,),
+    ("O", 0, 3, 1,),
+    ("G", 6, 3,),
+    ("O", 0, 0, 2,),
+    ("O", 0, 3, 2,),
+    ("O", 0, 1, 1,),
+    ("G", 7, 1,),
+    ("G", 7, 2,),
+    ("G", 7, 3,),
+    ("O", 0, 2, 2,),
+    ("qe", 3,),
+    ("O", 0, 0, 3,),
+    ("qe", 5,),
+    ("qe", 4,),
+    ("O", 0, 3, 3,),
+    ("O", 0, 1, 2,),
+    ("O", 0, 2, 3,),
+    ("il", 6, 0,),
+    ("il", 6, 1,),
+    ("O", 1, 0, 0,),
+    ("F", 0, 0, False,),
+    ("O", 1, 1, 0,),
+    ("O", 0, 1, 3,),
+    ("O", 1, 1, 1,),
+    ("O", 1, 3, 0,),
+    ("il", 7, 0,),
+    ("qe", 6,),
+    ("O", 1, 0, 1,),
+    ("F", 0, 3, False,),
+    ("O", 1, 0, 2,),
+    ("il", 7, 1,),
+    ("O", 1, 2, 0,),
+    ("O", 1, 1, 2,),
+    ("O", 1, 3, 1,),
+    ("qe", 7,),
+    ("O", 1, 0, 3,),
+    ("O", 1, 1, 3,),
+    ("F", 0, 2, False,),
+    ("O", 1, 3, 2,),
+    ("O", 1, 3, 3,),
+    ("F", 0, 1, False,),
+    ("O", 1, 2, 1,),
+    ("F", 1, 0, True,),
+    ("O", 1, 2, 2,),
+    ("F", 1, 1, False,),
+    ("F", 1, 3, False,),
+    ("O", 1, 2, 3,),
+    ("F", 1, 2, True,),
+]
 FLOPS = 2 * (M * N * D + N * F * C + M * N * C)
 
 F32 = mybir.dt.float32
@@ -36,7 +169,7 @@ def tile_balanced_nonlocal_means_s12_kernel(
         def kept(name, shape, dtype):
             return keep.tile(shape, dtype, name=name, tag=name, align_bytes=64)
 
-        a_codes = kept("a_codes", [P, DG, 2 * M], U8)
+        a_codes = [kept("a_codes%d" % h, [P, DG, 1024], U8) for h in range(2)]
         a_plane = kept("a_plane", [P, DG, M], U8)
         b_plane_raw = kept("b_plane_raw", [P, DG, N], U8)
         b_raw = [kept("b_raw%d" % g, [P, DG, 1024], U8) for g in range(JG)]
@@ -69,52 +202,52 @@ def tile_balanced_nonlocal_means_s12_kernel(
         sgn = kept("sgn", [P, JG, 4], F32)
         rho_col = kept("rho_col", [P, M // P], F32)
 
-        def load_b(g):
-            nc.sync.dma_start(
+        def load_b(queue, g):
+            queue.dma_start(
                 out=b_raw[g][:].bitcast(I32),
                 in_=b_words.rearrange("d p n -> p d n")[:, :, g * 1024 : (g + 1) * 1024].bitcast(I32),
             )
 
-        def load_a(h):
-            nc.sync.dma_start(
-                out=a_codes[:, :, h * 1024 : (h + 1) * 1024].bitcast(I32),
+        def load_a(queue, h):
+            queue.dma_start(
+                out=a_codes[h][:].bitcast(I32),
                 in_=a_words.rearrange("d p n -> p d n")[:, :, h * 1024 : (h + 1) * 1024].bitcast(I32),
             )
 
         def load_x(g):
             nc.sync.dma_start(out=x_raw[g][:], in_=x.rearrange("(g m b) f -> g m b f", g=JG, b=4)[g])
 
-        nc.gpsimd.dma_start(out=g_row[:], in_=gamma.rearrange("(g n) -> g n", g=JG))
-        nc.vector.memset(b_plane_raw[:].bitcast(I32), 0)
+        nc.sync.dma_start(out=g_row[:], in_=gamma.rearrange("(g n) -> g n", g=JG))
         make_identity(nc, id_bf[:])
         nc.vector.memset(a_plane[:].bitcast(I32), 0)
-        nc.vector.memset(vec_rows[:], 0.0)
+        nc.vector.memset(b_plane_raw[:].bitcast(I32), 0)
         nc.vector.memset(dummy[:], 1.0)
+        nc.vector.memset(vec_rows[:], 0.0)
         nc.vector.memset(rho_rows[:], 0.0)
+        nc.gpsimd.dma_start(out=rho_rows[0:8, :], in_=rho.rearrange("(i p) -> i p", p=P))
 
-        def load_plane(queue, plane, rows, q):
-            queue.dma_start(
+        def load_plane(plane, rows, q):
+            nc.sync.dma_start(
                 out=plane[32 * q : 32 * q + 4, :, :].bitcast(I32),
                 in_=rows[:, 4 * q : 4 * q + 4, :].rearrange("d r n -> r d n").bitcast(I32),
             )
 
+        for q in range(3):
+            load_plane(a_plane, a_scales, q)
         load_x(0)
-        load_b(0)
-        load_a(0)
+        load_b(nc.sync, 0)
+        load_a(nc.sync, 0)
+        load_plane(a_plane, a_scales, 3)
         for q in range(4):
-            load_plane(nc.scalar, b_plane_raw, b_scales, q)
-        load_plane(nc.scalar, a_plane, a_scales, 0)
-        for q in range(1, 4):
-            load_plane(nc.gpsimd, a_plane, a_scales, q)
-        nc.gpsimd.dma_start(out=rho_rows[0:8, :], in_=rho.rearrange("(i p) -> i p", p=P))
+            load_plane(b_plane_raw, b_scales, q)
         nc.sync.dma_start(out=w_raw[:], in_=w.rearrange("(p j) c -> p j c", j=4))
-        load_b(1)
-        load_b(2)
-        load_b(3)
+        load_b(nc.sync, 1)
+        load_b(nc.sync, 2)
         load_x(1)
+        load_b(nc.sync, 3)
         load_x(2)
         load_x(3)
-        load_a(1)
+        load_a(nc.sync, 1)
 
         nc.scalar.activation(out=mant_ln[:, 0, 0:1], in_=dummy[:], func=ACT.Ln)
         nc.vector.tensor_copy(out=id_f[:], in_=id_bf[:])
@@ -136,8 +269,8 @@ def tile_balanced_nonlocal_means_s12_kernel(
         v_grp = {}
         o_bank = {}
 
-        def turn_x(g, copy):
-            grp = work.tile([P, 512, 4], BF16, name="x_grp", tag="x_grp", bufs=2, align_bytes=64)
+        def turn_x(g):
+            grp = work.tile([P, 512, 4], BF16, name="x_grp", tag="x_grp", bufs=4, align_bytes=64)
             x_grp[g] = grp
             words = grp[:].rearrange("p c j -> p (c j)").bitcast(F32)
             banks = []
@@ -150,7 +283,7 @@ def tile_balanced_nonlocal_means_s12_kernel(
                             bank[:, 2 * bl + u, :], x_raw[g][:, 2 * k + bl, :].bitcast(F32)[:, u::2], id_f[:]
                         )
             for k in range(2):
-                copy(
+                nc.scalar.copy(
                     out=words.rearrange("p (t s e) -> p t s e", t=4, e=8)[:, :, :, 4 * k : 4 * k + 4],
                     in_=banks[k][:].rearrange("p e (s t) -> p t s e", t=4),
                 )
@@ -168,7 +301,7 @@ def tile_balanced_nonlocal_means_s12_kernel(
                     out=bank[:],
                     lhsT=b_codes[g][:, d, 256 * t : 256 * (t + 1)].bitcast(E2M1),
                     lhsT_scale=b_plane[g][:, d, P * t : P * (t + 1)],
-                    rhs=a_codes[:, d, 1024 * h : 1024 * (h + 1)].bitcast(E2M1),
+                    rhs=a_codes[h][:, d, :].bitcast(E2M1),
                     rhs_scale=a_plane[:, d, HALF * h : HALF * (h + 1)],
                     start=(d == 0),
                     stop=(d == DG - 1),
@@ -179,7 +312,7 @@ def tile_balanced_nonlocal_means_s12_kernel(
 
         def interleave(s, part):
             if part == 0:
-                e_grp[s] = work.tile([P, HALF, 4], BF16, name="e_grp", tag="e_grp", bufs=3, align_bytes=64)
+                e_grp[s] = work.tile([P, HALF, 4], BF16, name="e_grp", tag="e_grp", bufs=4, align_bytes=64)
             cols = slice(part * 256, (part + 1) * 256)
             nc.vector.tensor_copy(
                 out=e_grp[s][:, cols, :].rearrange("p (c i) t -> p c t i", i=4),
@@ -205,7 +338,7 @@ def tile_balanced_nonlocal_means_s12_kernel(
                     stop=True,
                 )
             if cq == 0:
-                v_grp[g] = work.tile([P, C, 4], BF16, name="v_grp", tag="v_grp", bufs=2, align_bytes=64)
+                v_grp[g] = work.tile([P, C, 4], BF16, name="v_grp", tag="v_grp", bufs=4, align_bytes=64)
             nc.vector.tensor_tensor(
                 out=v_grp[g][:, cols, :],
                 in0=bank[:].rearrange("p t c -> p c t"),
@@ -258,8 +391,6 @@ def tile_balanced_nonlocal_means_s12_kernel(
         )
         nc.scalar.activation(out=mant_ln[:], in_=mant[:].bitcast(F32), func=ACT.Ln)
         nc.scalar.activation(out=dummy[:], in_=dummy[:], func=ACT.Exp)
-        turn_x(0, nc.vector.tensor_copy)
-        arrange_b(0)
         nc.vector.tensor_scalar(
             out=expo_ln[:], in0=expo[:], scalar1=-127.0, scalar2=math.log(2.0), op0=ALU.add, op1=ALU.mult
         )
@@ -279,85 +410,26 @@ def tile_balanced_nonlocal_means_s12_kernel(
             nc.vector.quantize_mx(
                 out=w_codes[:].bitcast(E4M3), scales=w_plane[:], in_=w_grp[:].rearrange("p c j -> p (c j)")
             )
-        for t in range(4):
-            weigh(0, t)
-        quant_x(0)
-        weights_w()
-        arrange_b(1)
-        quant_w()
-        turn_x(1, nc.scalar.copy)
-        arrange_b(2)
-        rho_t = psum.tile([P, P], BF16, name="rho_t", tag="m", bufs=4)
-        nc.tensor.transpose(rho_t[:], rho_rows[:], id_bf[:])
-        nc.vector.tensor_copy(out=rho_col[:], in_=rho_t[:, 0:8])
-        interleave(0, 0)
-        for t in range(4):
-            weigh(1, t)
-        interleave(0, 1)
-        arrange_b(3)
-        quant_x(1)
-        turn_x(2, nc.scalar.copy)
-        quant_e(0)
-        for t in range(4):
-            weigh(2, t)
-            project(0, t)
-            if t == 0:
-                interleave(1, 0)
-            if t == 1:
-                interleave(1, 1)
-        quant_x(2)
-        quant_v(0)
-        turn_x(3, nc.scalar.copy)
-        for t in range(4):
-            weigh(3, t)
-            project(1, t)
-            if t == 0:
-                quant_e(1)
-        quant_x(3)
-        quant_v(1)
-        interleave(2, 0)
-        for t in range(4):
-            weigh(4, t)
-            project(2, t)
-        interleave(2, 1)
-        for t in range(4):
-            weigh(5, t)
-            project(3, t)
-        quant_v(2)
-        quant_e(2)
-        quant_v(3)
-        interleave(3, 0)
-        interleave(3, 1)
-        for t in range(4):
-            weigh(6, t)
-            average(0, t, 0)
-        interleave(4, 0)
-        quant_e(3)
-        for t in range(4):
-            average(0, t, 1)
-        interleave(4, 1)
-        for t in range(4):
-            weigh(7, t)
-            average(0, t, 2)
-        interleave(5, 0)
-        quant_e(4)
-        interleave(5, 1)
-        interleave(6, 0)
-        quant_e(5)
-        interleave(6, 1)
-        for t in range(4):
-            average(0, t, 3)
-            finish(0, t, False)
-        interleave(7, 0)
-        quant_e(6)
-        interleave(7, 1)
-        for i in range(4):
-            for g in range(3):
-                average(1, i, g)
-            if i == 1:
-                quant_e(7)
-            if i > 0:
-                average(1, i - 1, 3)
-                finish(1, i - 1, i % 2 == 1)
-        average(1, 3, 3)
-        finish(1, 3, False)
+
+        def rho_turn():
+            rho_t = psum.tile([P, P], BF16, name="rho_t", tag="m", bufs=4)
+            nc.tensor.transpose(rho_t[:], rho_rows[:], id_bf[:])
+            nc.vector.tensor_copy(out=rho_col[:], in_=rho_t[:, 0:8])
+
+        do = {
+            "G": weigh,
+            "T": turn_x,
+            "V": project,
+            "O": average,
+            "F": finish,
+            "arr": arrange_b,
+            "il": interleave,
+            "qe": quant_e,
+            "qx": quant_x,
+            "qv": quant_v,
+            "wi": weights_w,
+            "wq": quant_w,
+            "rho": rho_turn,
+        }
+        for step in PLAN:
+            do[step[0]](*step[1:])

import math
from contextlib import ExitStack

import concourse.mybir as mybir
from concourse.masks import make_identity

M, N, D, F, C = 1024, 2048, 1024, 512, 512
PLAN = [
    ("T", 0,),
    ("rho",),
    ("arr", 0,),
    ("G", 0, 0,),
    ("qx", 0,),
    ("arr", 1,),
    ("G", 0, 1,),
    ("G", 0, 2,),
    ("G", 0, 3,),
    ("wi",),
    ("G", 1, 0,),
    ("G", 1, 1,),
    ("il", 0, 0,),
    ("G", 1, 2,),
    ("G", 1, 3,),
    ("arr", 2,),
    ("T", 1,),
    ("arr", 3,),
    ("T", 2,),
    ("wq",),
    ("il", 1, 0,),
    ("il", 0, 1,),
    ("qx", 1,),
    ("V", 0, 0,),
    ("G", 2, 0,),
    ("il", 1, 1,),
    ("G", 2, 1,),
    ("V", 1, 0,),
    ("V", 1, 1,),
    ("qe", 1,),
    ("G", 3, 0,),
    ("V", 0, 1,),
    ("G", 2, 2,),
    ("qx", 2,),
    ("G", 2, 3,),
    ("V", 0, 2,),
    ("V", 1, 2,),
    ("V", 0, 3,),
    ("T", 3,),
    ("G", 4, 0,),
    ("qe", 0,),
    ("G", 3, 1,),
    ("qv", 0,),
    ("il", 2, 0,),
    ("G", 3, 2,),
    ("qx", 3,),
    ("V", 1, 3,),
    ("G", 3, 3,),
    ("V", 2, 0,),
    ("qv", 1,),
    ("G", 4, 1,),
    ("V", 2, 1,),
    ("V", 3, 0,),
    ("G", 4, 2,),
    ("il", 3, 0,),
    ("G", 4, 3,),
    ("O", 0, 2, 0,),
    ("V", 2, 2,),
    ("O", 0, 3, 0,),
    ("V", 3, 1,),
    ("il", 2, 1,),
    ("G", 5, 0,),
    ("V", 3, 2,),
    ("il", 4, 0,),
    ("O", 0, 2, 1,),
    ("O", 0, 0, 0,),
    ("G", 6, 0,),
    ("V", 2, 3,),
    ("G", 5, 1,),
    ("O", 0, 1, 0,),
    ("il", 3, 1,),
    ("O", 0, 0, 1,),
    ("G", 7, 0,),
    ("G", 5, 2,),
    ("G", 5, 3,),
    ("qv", 2,),
    ("il", 4, 1,),
    ("qe", 2,),
    ("V", 3, 3,),
    ("il", 5, 0,),
    ("G", 6, 1,),
    ("il", 5, 1,),
    ("qv", 3,),
    ("G", 6, 2,),
    ("O", 0, 3, 1,),
    ("G", 6, 3,),
    ("O", 0, 0, 2,),
    ("O", 0, 3, 2,),
    ("O", 0, 1, 1,),
    ("G", 7, 1,),
    ("G", 7, 2,),
    ("G", 7, 3,),
    ("O", 0, 2, 2,),
    ("qe", 3,),
    ("O", 0, 0, 3,),
    ("qe", 5,),
    ("qe", 4,),
    ("O", 0, 3, 3,),
    ("O", 0, 1, 2,),
    ("O", 0, 2, 3,),
    ("il", 6, 0,),
    ("il", 6, 1,),
    ("O", 1, 0, 0,),
    ("F", 0, 0, False,),
    ("O", 1, 1, 0,),
    ("O", 0, 1, 3,),
    ("O", 1, 1, 1,),
    ("O", 1, 3, 0,),
    ("il", 7, 0,),
    ("qe", 6,),
    ("O", 1, 0, 1,),
    ("F", 0, 3, False,),
    ("O", 1, 0, 2,),
    ("il", 7, 1,),
    ("O", 1, 2, 0,),
    ("O", 1, 1, 2,),
    ("O", 1, 3, 1,),
    ("qe", 7,),
    ("O", 1, 0, 3,),
    ("O", 1, 1, 3,),
    ("F", 0, 2, False,),
    ("O", 1, 3, 2,),
    ("O", 1, 3, 3,),
    ("F", 0, 1, False,),
    ("O", 1, 2, 1,),
    ("F", 1, 0, True,),
    ("O", 1, 2, 2,),
    ("F", 1, 1, False,),
    ("F", 1, 3, False,),
    ("O", 1, 2, 3,),
    ("F", 1, 2, True,),
]
FLOPS = 2 * (M * N * D + N * F * C + M * N * C)

F32 = mybir.dt.float32
BF16 = mybir.dt.bfloat16
I32 = mybir.dt.int32
U32 = mybir.dt.uint32
U8 = mybir.dt.uint8
E4M3 = mybir.dt.float8_e4m3fn_x4
E2M1 = mybir.dt.float4_e2m1fn_x4
ALU = mybir.AluOpType
ACT = mybir.ActivationFunctionType

P = 128
JG = N // 512
HALF = 512
DG = D // 512


def tile_balanced_nonlocal_means_s12_kernel(
    tc, a_words, a_scales, b_words, b_scales, gamma, rho, x, w, out
):
    nc = tc.nc
    with ExitStack() as ctx:
        keep = ctx.enter_context(tc.tile_pool(name="keep", bufs=1))
        work = ctx.enter_context(tc.tile_pool(name="work", bufs=3))
        psum = ctx.enter_context(tc.psum_pool(name="psum", bufs=4))
        ctx.enter_context(tc.manual_schedule())

        def kept(name, shape, dtype):
            return keep.tile(shape, dtype, name=name, tag=name, align_bytes=64)

        a_codes = [kept("a_codes%d" % h, [P, DG, 1024], U8) for h in range(2)]
        a_plane = kept("a_plane", [P, DG, M], U8)
        b_plane_raw = kept("b_plane_raw", [P, DG, N], U8)
        b_raw = [kept("b_raw%d" % g, [P, DG, 1024], U8) for g in range(JG)]
        b_codes = [kept("b_codes%d" % g, [P, DG, 1024], U8) for g in range(JG)]
        b_plane = [kept("b_plane%d" % g, [P, DG, 512], U8) for g in range(JG)]
        x_raw = [kept("x_raw%d" % g, [P, 4, F], BF16) for g in range(JG)]
        w_raw = kept("w_raw", [P, 4, C], BF16)
        w_grp = kept("w_grp", [P, C, 4], BF16)
        w_codes = kept("w_codes", [P, C], U32)
        w_plane = kept("w_plane", [P, C], U8)
        x_codes = [kept("x_codes%d" % g, [P, 512], U32) for g in range(JG)]
        x_plane = [kept("x_plane%d" % g, [P, 512], U8) for g in range(JG)]
        v_codes = [kept("v_codes%d" % g, [P, C], U32) for g in range(JG)]
        v_plane = [kept("v_plane%d" % g, [P, C], U8) for g in range(JG)]
        e_codes = [kept("e_codes%d" % s, [P, HALF], U32) for s in range(2 * JG)]
        e_plane = [kept("e_plane%d" % s, [P, HALF], U8) for s in range(2 * JG)]
        g_row = kept("g_row", [JG, 512], BF16)
        vec_rows = kept("vec_rows", [P, 4, P], BF16)
        rho_rows = kept("rho_rows", [P, P], BF16)
        id_bf = kept("id_bf", [P, P], BF16)
        id_f = kept("id_f", [P, P], F32)
        dummy = kept("dummy", [P, 1], F32)
        gam = kept("gam", [P, 4, JG], F32)
        mant = kept("mant", [P, 4, JG], I32)
        expo = kept("expo", [P, 4, JG], I32)
        expo_ln = kept("expo_ln", [P, 4, JG], F32)
        mant_ln = kept("mant_ln", [P, 4, JG], F32)
        ln_gam = kept("ln_gam", [P, 4, JG], F32)
        sgn2 = kept("sgn2", [P, JG, 4], F32)
        sgn = kept("sgn", [P, JG, 4], F32)
        rho_col = kept("rho_col", [P, M // P], F32)

        def load_b(queue, g):
            queue.dma_start(
                out=b_raw[g][:].bitcast(I32),
                in_=b_words.rearrange("d p n -> p d n")[:, :, g * 1024 : (g + 1) * 1024].bitcast(I32),
            )

        def load_a(queue, h):
            queue.dma_start(
                out=a_codes[h][:].bitcast(I32),
                in_=a_words.rearrange("d p n -> p d n")[:, :, h * 1024 : (h + 1) * 1024].bitcast(I32),
            )

        def load_x(g):
            nc.sync.dma_start(out=x_raw[g][:], in_=x.rearrange("(g m b) f -> g m b f", g=JG, b=4)[g])

        nc.sync.dma_start(out=g_row[:], in_=gamma.rearrange("(g n) -> g n", g=JG))
        make_identity(nc, id_bf[:])
        nc.vector.memset(a_plane[:].bitcast(I32), 0)
        nc.vector.memset(b_plane_raw[:].bitcast(I32), 0)
        nc.vector.memset(dummy[:], 1.0)
        nc.vector.memset(vec_rows[:], 0.0)
        nc.vector.memset(rho_rows[:], 0.0)
        nc.gpsimd.dma_start(out=rho_rows[0:8, :], in_=rho.rearrange("(i p) -> i p", p=P))

        def load_plane(plane, rows, q):
            nc.sync.dma_start(
                out=plane[32 * q : 32 * q + 4, :, :].bitcast(I32),
                in_=rows[:, 4 * q : 4 * q + 4, :].rearrange("d r n -> r d n").bitcast(I32),
            )

        for q in range(3):
            load_plane(a_plane, a_scales, q)
        load_x(0)
        load_b(nc.sync, 0)
        load_a(nc.sync, 0)
        load_plane(a_plane, a_scales, 3)
        for q in range(4):
            load_plane(b_plane_raw, b_scales, q)
        nc.sync.dma_start(out=w_raw[:], in_=w.rearrange("(p j) c -> p j c", j=4))
        load_b(nc.sync, 1)
        load_b(nc.sync, 2)
        load_x(1)
        load_b(nc.sync, 3)
        load_x(2)
        load_x(3)
        load_a(nc.sync, 1)

        nc.scalar.activation(out=mant_ln[:, 0, 0:1], in_=dummy[:], func=ACT.Ln)
        nc.vector.tensor_copy(out=id_f[:], in_=id_bf[:])

        def arrange_b(g):
            for d in range(DG):
                nc.vector.tensor_copy(
                    out=b_codes[g][:, d, :].bitcast(I32).rearrange("p (t s w) -> p t s w", t=4, w=2),
                    in_=b_raw[g][:, d, :].bitcast(I32).rearrange("p (s t w) -> p t s w", t=4, w=2),
                )
            nc.vector.tensor_copy(
                out=b_plane[g][:].bitcast(I32).rearrange("p d (t s) -> p d t s", t=4),
                in_=b_plane_raw[:, :, g * 512 : (g + 1) * 512].bitcast(I32).rearrange("p d (s t) -> p d t s", t=4),
            )

        x_grp = {}
        e_bf = {}
        e_grp = {}
        v_grp = {}
        o_bank = {}

        def turn_x(g):
            grp = work.tile([P, 512, 4], BF16, name="x_grp", tag="x_grp", bufs=4, align_bytes=64)
            x_grp[g] = grp
            words = grp[:].rearrange("p c j -> p (c j)").bitcast(F32)
            banks = []
            for k in range(2):
                bank = psum.tile([P, 4, P], F32, name="xt", tag="m", bufs=4)
                banks.append(bank)
                for bl in range(2):
                    for u in range(2):
                        nc.tensor.transpose(
                            bank[:, 2 * bl + u, :], x_raw[g][:, 2 * k + bl, :].bitcast(F32)[:, u::2], id_f[:]
                        )
            for k in range(2):
                nc.scalar.copy(
                    out=words.rearrange("p (t s e) -> p t s e", t=4, e=8)[:, :, :, 4 * k : 4 * k + 4],
                    in_=banks[k][:].rearrange("p e (s t) -> p t s e", t=4),
                )

        def quant_x(g):
            nc.vector.quantize_mx(
                out=x_codes[g][:].bitcast(E4M3), scales=x_plane[g][:], in_=x_grp[g][:].rearrange("p c j -> p (c j)")
            )

        def weigh(s, t):
            h, g = divmod(s, JG)
            bank = psum.tile([P, HALF], F32, name="gram", tag="m", bufs=4)
            for d in range(DG):
                nc.tensor.matmul_mx(
                    out=bank[:],
                    lhsT=b_codes[g][:, d, 256 * t : 256 * (t + 1)].bitcast(E2M1),
                    lhsT_scale=b_plane[g][:, d, P * t : P * (t + 1)],
                    rhs=a_codes[h][:, d, :].bitcast(E2M1),
                    rhs_scale=a_plane[:, d, HALF * h : HALF * (h + 1)],
                    start=(d == 0),
                    stop=(d == DG - 1),
                )
            if t == 0:
                e_bf[s] = work.tile([P, 4, HALF], BF16, name="e_bf", tag="e_bf", bufs=8, align_bytes=64)
            nc.scalar.activation(out=e_bf[s][:, t, :], in_=bank[:], func=ACT.Exp, bias=ln_gam[:, t, g : g + 1])

        def interleave(s, part):
            if part == 0:
                e_grp[s] = work.tile([P, HALF, 4], BF16, name="e_grp", tag="e_grp", bufs=4, align_bytes=64)
            cols = slice(part * 256, (part + 1) * 256)
            nc.vector.tensor_copy(
                out=e_grp[s][:, cols, :].rearrange("p (c i) t -> p c t i", i=4),
                in_=e_bf[s][:, :, cols].rearrange("p t (c i) -> p c t i", i=4),
            )

        def quant_e(s):
            nc.vector.quantize_mx(
                out=e_codes[s][:].bitcast(E4M3), scales=e_plane[s][:], in_=e_grp[s][:].rearrange("p c t -> p (c t)")
            )

        def project(g, cq):
            bank = psum.tile([P, 4, P], F32, name="val", tag="m", bufs=4)
            cols = slice(P * cq, P * (cq + 1))
            for t in range(4):
                nc.tensor.matmul_mx(
                    out=bank[:, t, :],
                    lhsT=x_codes[g][:, P * t : P * (t + 1)].bitcast(E4M3),
                    lhsT_scale=x_plane[g][:, P * t : P * (t + 1)],
                    rhs=w_codes[:, cols].bitcast(E4M3),
                    rhs_scale=w_plane[:, cols],
                    start=True,
                    stop=True,
                )
            if cq == 0:
                v_grp[g] = work.tile([P, C, 4], BF16, name="v_grp", tag="v_grp", bufs=4, align_bytes=64)
            nc.vector.tensor_tensor(
                out=v_grp[g][:, cols, :],
                in0=bank[:].rearrange("p t c -> p c t"),
                in1=sgn[:, g : g + 1, :].to_broadcast([P, P, 4]),
                op=ALU.mult,
            )

        def quant_v(g):
            nc.vector.quantize_mx(
                out=v_codes[g][:].bitcast(E4M3), scales=v_plane[g][:], in_=v_grp[g][:].rearrange("p c t -> p (c t)")
            )

        def average(h, i, g):
            if g == 0:
                o_bank[h, i] = psum.tile([P, C], F32, name="avg", tag=("o", "m")[h], bufs=4)
            s = h * JG + g
            nc.tensor.matmul_mx(
                out=o_bank[h, i][:],
                lhsT=e_codes[s][:, P * i : P * (i + 1)].bitcast(E4M3),
                lhsT_scale=e_plane[s][:, P * i : P * (i + 1)],
                rhs=v_codes[g][:].bitcast(E4M3),
                rhs_scale=v_plane[g][:],
                start=(g == 0),
                stop=(g == JG - 1),
            )

        def finish(h, i, on_vector):
            k = 4 * h + i
            res = work.tile([P, C], F32, name="res", tag="res", bufs=4)
            if on_vector:
                nc.vector.tensor_scalar_mul(out=res[:], in0=o_bank[h, i][:], scalar1=rho_col[:, k : k + 1])
            else:
                nc.scalar.activation(out=res[:], in_=o_bank[h, i][:], func=ACT.Copy, scale=rho_col[:, k : k + 1])
            nc.sync.dma_start(out=out[P * k : P * (k + 1), :], in_=res[:])

        nc.vector.tensor_copy(
            out=vec_rows[0:JG, :, :].rearrange("g t (s b) -> g t s b", b=4),
            in_=g_row[:].rearrange("g (s t b) -> g t s b", t=4, b=4),
        )
        vec_t = psum.tile([P, 4, P], BF16, name="vec_t", tag="m", bufs=4)
        for t in range(4):
            nc.tensor.transpose(vec_t[:, t, :], vec_rows[:, t, :], id_bf[:])
        nc.vector.tensor_copy(out=gam[:], in_=vec_t[:, :, 0:JG])
        bits = gam[:].bitcast(I32)
        nc.vector.tensor_scalar(
            out=mant[:], in0=bits, scalar1=0x007FFFFF, scalar2=0x3F800000, op0=ALU.bitwise_and, op1=ALU.bitwise_or
        )
        nc.vector.tensor_scalar(
            out=expo[:], in0=bits, scalar1=23, scalar2=0xFF, op0=ALU.logical_shift_right, op1=ALU.bitwise_and
        )
        nc.scalar.activation(out=mant_ln[:], in_=mant[:].bitcast(F32), func=ACT.Ln)
        nc.scalar.activation(out=dummy[:], in_=dummy[:], func=ACT.Exp)
        nc.vector.tensor_scalar(
            out=expo_ln[:], in0=expo[:], scalar1=-127.0, scalar2=math.log(2.0), op0=ALU.add, op1=ALU.mult
        )
        nc.vector.tensor_scalar(
            out=sgn2[:], in0=gam[:].rearrange("p t g -> p g t"), scalar1=0.0, scalar2=2.0, op0=ALU.is_ge, op1=ALU.mult
        )
        nc.vector.tensor_tensor(out=ln_gam[:], in0=mant_ln[:], in1=expo_ln[:], op=ALU.add)
        nc.vector.tensor_scalar_add(out=sgn[:], in0=sgn2[:], scalar1=-1.0)


        def weights_w():
            nc.vector.tensor_copy(
                out=w_grp[:].rearrange("p (c i) j -> p c j i", i=4), in_=w_raw[:].rearrange("p j (c i) -> p c j i", i=4)
            )

        def quant_w():
            nc.vector.quantize_mx(
                out=w_codes[:].bitcast(E4M3), scales=w_plane[:], in_=w_grp[:].rearrange("p c j -> p (c j)")
            )

        def rho_turn():
            rho_t = psum.tile([P, P], BF16, name="rho_t", tag="m", bufs=4)
            nc.tensor.transpose(rho_t[:], rho_rows[:], id_bf[:])
            nc.vector.tensor_copy(out=rho_col[:], in_=rho_t[:, 0:8])

        do = {
            "G": weigh,
            "T": turn_x,
            "V": project,
            "O": average,
            "F": finish,
            "arr": arrange_b,
            "il": interleave,
            "qe": quant_e,
            "qx": quant_x,
            "qv": quant_v,
            "wi": weights_w,
            "wq": quant_w,
            "rho": rho_turn,
        }
        for step in PLAN:
            do[step[0]](*step[1:])
